import numpy as np
import ml_dtypes


def mxq(x, axis, fmt="e4m3"):
    dtype, down = {"e4m3": (ml_dtypes.float8_e4m3fn, 7), "e5m2": (ml_dtypes.float8_e5m2, 14)}[fmt]
    v = np.moveaxis(np.asarray(x, np.float32).astype(ml_dtypes.bfloat16).astype(np.float64), axis, -1)
    blocks = v.reshape(v.shape[:-1] + (-1, 32))
    amax = np.abs(blocks).max(-1, keepdims=True)
    byte = np.maximum(np.where(amax > 0, np.frexp(amax)[1] - 1 + 127, 0) - down, 1)
    scale = np.exp2(byte - 127.0)
    codes = (blocks / scale).astype(np.float32).astype(dtype).astype(np.float64)
    return np.moveaxis((codes * scale).reshape(v.shape), -1, axis)


WIDE = False


def mx_kscale(k):
    if not WIDE:
        return np.ones(k)
    levels = np.array([10, -10, 5, -5, 0])
    if k % 512:
        return np.exp2(np.random.permutation(np.resize(levels, k // 32))).repeat(32)
    a = np.empty((k // 512, 16))
    for p in range(k // 512):
        a[p, :8] = np.random.permutation(np.resize(levels, 8))
        for g in range(8):
            far = levels[np.abs(levels - a[p, g]) >= 10]
            a[p, g + 8] = far[np.random.randint(len(far))]
    return np.exp2(a.ravel()).repeat(32)


def f64(x):
    return np.asarray(x).astype(np.float64)


def striped(idx):
    return np.tile(idx.reshape(-1, 16).T, (8, 1)).astype(np.uint16)


def unstriped(offs):
    return offs[:16].T.reshape(-1).astype(np.int64)


def gelu(v):
    return 0.5 * v * (1.0 + np.tanh(np.sqrt(2.0 / np.pi) * (v + 0.044715 * v**3)))


K, T, E, C, H, N = 1536, 1280, 4, 256, 512, 256


def by_expert(wq, xq):
    return np.concatenate([wq[e].T @ xq[:, e * C:(e + 1) * C] for e in range(E)], axis=1)


def setup_inputs():
    n = np.random.standard_normal
    s = mx_kscale(K)[:, None]
    u = mx_kscale(H)
    return {
        "xT": (n((K, T)) * s).astype(np.float32),
        "xr": n((N, T)).astype(np.float32),
        "w1": (n((E, K, H)) / np.sqrt(K) / s[None] * u[None, None, :]).astype(np.float32),
        "w2": (n((E, H, N)) / np.sqrt(H) / u[None, :, None]).astype(np.float32),
        "gate": np.tile(np.random.uniform(0.2, 1.0, E * C), (N, 1)).astype(np.float32),
        "offs": striped(np.random.permutation(T)[:E * C]),
    }


def reference(xT, xr, w1, w2, gate, offs):
    idx = unstriped(offs)
    xq = mxq(f64(xT)[:, idx], 0, "e4m3")
    h = gelu(by_expert(mxq(f64(w1), 1, "e4m3"), xq))
    y = by_expert(mxq(f64(w2), 1, "e4m3"), mxq(h, 0, "e4m3"))
    out = f64(xr).copy()
    out[:, idx] += f64(gate) * y
    return out

@@ -1,0 +1,218 @@
+from contextlib import ExitStack
+
+import concourse.mybir as mybir
+
+K, T, E, C, H, N = 1536, 1280, 4, 256, 512, 256
+S = E * C
+
+FLOPS = 2 * S * K * H + 2 * S * H * N
+BYTES = 4 * (K * T + 2 * N * T + E * K * H + E * H * N + 128 * S) + 2 * 128 * (S // 16)
+
+F32 = mybir.dt.float32
+BF16 = mybir.dt.bfloat16
+U32 = mybir.dt.uint32
+U16 = mybir.dt.uint16
+U8 = mybir.dt.uint8
+FP8X4 = mybir.dt.float8_e4m3fn_x4
+COPY = mybir.ActivationFunctionType.Copy
+GELU = mybir.ActivationFunctionType.Gelu_apprx_tanh
+MULT = mybir.AluOpType.mult
+ADD = mybir.AluOpType.add
+
+P = 128
+PASSES = K // 512
+X_CHUNKS = ((0, 256), (256, 512), (768, 512))
+X_VECTOR = 1 / 8
+W1_VECTOR = 32
+W2_VECTOR = 64
+RAW_BUFS = 11
+LIST_HALF = 512
+
+
+def tile_moe_res_mlp_gelu_kernel(tc, xT, xr, w1, w2, gate, offs, out):
+    nc = tc.nc
+    with ExitStack() as ctx:
+        keep = ctx.enter_context(tc.tile_pool(name="keep", bufs=1))
+        raw_pool = ctx.enter_context(tc.tile_pool(name="raw_pool", bufs=RAW_BUFS))
+        stage = ctx.enter_context(tc.tile_pool(name="stage", bufs=4))
+        w_pool = ctx.enter_context(tc.tile_pool(name="w_pool", bufs=8))
+        w2_pool = ctx.enter_context(tc.tile_pool(name="w2_pool", bufs=2))
+        small = ctx.enter_context(tc.tile_pool(name="small", bufs=3))
+        psum1 = ctx.enter_context(tc.psum_pool(name="psum1", bufs=4))
+        psum2 = ctx.enter_context(tc.psum_pool(name="psum2", bufs=3))
+
+        offsets = keep.tile([P, S // 16], U16, name="offsets")
+        nc.sync.dma_start(offsets[:], offs)
+
+        warm = keep.tile([P, 2], F32, name="warm")
+        nc.vector.memset(warm[:], 0.0)
+        nc.scalar.activation(out=warm[:, 1:2], in_=warm[:, 0:1], func=GELU)
+
+        x_scales = keep.tile([P, T], U8, name="x_scales", align_bytes=64)
+        nc.gpsimd.memset(x_scales[:], 0)
+        sums = [keep.tile([P, T], F32, name=f"sums{b}") for b in range(2)]
+        for b in range(2):
+            nc.vector.memset(sums[b][:], 0.0)
+
+        x_codes = [keep.tile([P, T], U32, name=f"x_codes{s}", align_bytes=64) for s in range(PASSES)]
+        g_codes = [
+            [keep.tile([P, LIST_HALF], U32, name=f"g_codes{s}_{f}", align_bytes=64) for f in range(2)]
+            for s in range(PASSES)
+        ]
+        g_scales = [keep.tile([P, LIST_HALF], U8, name=f"g_scales{f}", align_bytes=64) for f in range(2)]
+        gates = keep.tile([P, S], F32, name="gates")
+        residual = [keep.tile([P, T], F32, name=f"residual{b}") for b in range(2)]
+        final = [keep.tile([P, T], F32, name=f"final{b}") for b in range(2)]
+
+        loaded = {}
+
+        def load_x(s, chunk):
+            c0, width = X_CHUNKS[chunk]
+            raw = raw_pool.tile([P, 4, width], F32, name="raw", align_bytes=64)
+            rows = xT[512 * s : 512 * (s + 1), c0 : c0 + width]
+            nc.sync.dma_start(out=raw[:], in_=rows.rearrange("(p j) w -> p j w", j=4))
+            loaded["x", s, chunk] = raw
+
+        def load_w1(e, s):
+            raw = raw_pool.tile([P, 4, H], F32, name="raw", align_bytes=64)
+            rows = w1[e, 512 * s : 512 * (s + 1), :]
+            nc.sync.dma_start(out=raw[:], in_=rows.rearrange("(p j) w -> p j w", j=4))
+            loaded["w1", e, s] = raw
+
+        def load_w2(e):
+            raw = w2_pool.tile([P, 4, N], F32, name="raw2", align_bytes=64)
+            nc.sync.dma_start(out=raw[:], in_=w2[e].rearrange("(p j) w -> p j w", j=4))
+            loaded["w2", e] = raw
+
+        def load_gate():
+            nc.sync.dma_start(out=gates[:], in_=gate[0:P, :])
+
+        def load_xr(b):
+            nc.sync.dma_start(out=residual[b][:], in_=xr[P * b : P * (b + 1), :])
+
+        loads = []
+        for s in range(PASSES):
+            for chunk in range(3):
+                loads.append((load_x, s, chunk))
+        for e in range(E):
+            for s in range(PASSES):
+                loads.append((load_w1, e, s))
+            loads.append((load_w2, e))
+            if e == 0:
+                loads.append((load_gate,))
+        loads.append((load_xr, 0))
+        loads.append((load_xr, 1))
+        loads.reverse()
+
+        def issue(count):
+            for i in range(min(count, len(loads))):
+                call = loads.pop()
+                call[0](*call[1:])
+
+        def split_copy(dst, src, cut):
+            if cut > 0:
+                nc.vector.tensor_copy(out=dst[:, :cut], in_=src[:, :cut])
+            nc.scalar.activation(out=dst[:, cut:], in_=src[:, cut:], func=COPY)
+
+        def quantize(codes, scales, grouped):
+            nc.vector.quantize_mx(out=codes.bitcast(FP8X4), scales=scales, in_=grouped)
+
+        issue(RAW_BUFS - 1)
+        for s in range(PASSES):
+            for chunk in range(3):
+                c0, width = X_CHUNKS[chunk]
+                raw = loaded.pop(("x", s, chunk))
+                grouped = stage.tile([P, 4 * width], BF16, name="grouped", align_bytes=64)
+                split_copy(
+                    grouped[:].rearrange("p (c i t) -> p c t i", i=4, t=4),
+                    raw[:].rearrange("p t (c i) -> p c t i", i=4),
+                    int(width // 4 * X_VECTOR),
+                )
+                quantize(x_codes[s][:, c0 : c0 + width], x_scales[4 * s : P, c0 : c0 + width], grouped[:])
+                issue(1)
+            for f in range(2):
+                picked = offsets[:, 32 * f : 32 * (f + 1)]
+                nc.vector.tensor_copy(g_codes[s][f][:], x_codes[s][:].indirect(picked))
+        for f in range(2):
+            picked = offsets[:, 32 * f : 32 * (f + 1)]
+            nc.vector.tensor_copy(g_scales[f][:], x_scales[:].indirect(picked))
+
+        for e in range(E):
+            w1_codes = []
+            w1_scales = []
+            for s in range(PASSES):
+                raw = loaded.pop(("w1", e, s))
+                grouped = stage.tile([P, 4 * H], BF16, name="grouped", align_bytes=64)
+                split_copy(
+                    grouped[:].rearrange("p (t m j) -> p m j t", t=4, j=4),
+                    raw[:].rearrange("p j (m t) -> p m j t", t=4),
+                    W1_VECTOR,
+                )
+                codes = w_pool.tile([P, H], U32, name="w1_codes", align_bytes=64)
+                scales = w_pool.tile([P, H], U8, name="w1_scales", align_bytes=64)
+                quantize(codes[:], scales[:], grouped[:])
+                w1_codes.append(codes)
+                w1_scales.append(scales)
+                issue(1)
+            raw = loaded.pop(("w2", e))
+            grouped2 = stage.tile([P, 4 * N], BF16, name="grouped2", align_bytes=64)
+            split_copy(
+                grouped2[:].rearrange("p (c i j) -> p c j i", i=4, j=4),
+                raw[:].rearrange("p j (c i) -> p c j i", i=4),
+                W2_VECTOR // 4,
+            )
+            w2_codes = w2_pool.tile([P, N], U32, name="w2_codes", align_bytes=64)
+            w2_scales = w2_pool.tile([P, N], U8, name="w2_scales", align_bytes=64)
+            quantize(w2_codes[:], w2_scales[:], grouped2[:])
+            issue(2)
+
+            y_bank = psum2.tile([P, 2, C], F32, name="y_bank")
+            h_codes = small.tile([P, C], U32, name="h_codes", align_bytes=64)
+            h_scales = small.tile([P, C], U8, name="h_scales", align_bytes=64)
+            for part in range(2):
+                slot = C * e + 128 * part
+                f, at = divmod(slot, LIST_HALF)
+                a_bank = psum1.tile([P, 4, 128], F32, name="a_bank")
+                for t in range(4):
+                    for s in range(PASSES):
+                        nc.tensor.matmul_mx(
+                            out=a_bank[:, t, :],
+                            lhsT=w1_codes[s][:, 128 * t : 128 * (t + 1)].bitcast(FP8X4),
+                            lhsT_scale=w1_scales[s][:, 128 * t : 128 * (t + 1)],
+                            rhs=g_codes[s][f][:, at : at + 128].bitcast(FP8X4),
+                            rhs_scale=g_scales[f][4 * s : P, at : at + 128],
+                            start=(s == 0),
+                            stop=(s == PASSES - 1),
+                        )
+                hidden = small.tile([P, 512], BF16, name="hidden", align_bytes=64)
+                nc.scalar.activation(
+                    out=hidden[:].rearrange("p (n t) -> p n t", t=4),
+                    in_=a_bank[:].rearrange("p t n -> p n t"),
+                    func=GELU,
+                )
+                cols = slice(128 * part, 128 * (part + 1))
+                quantize(h_codes[:, cols], h_scales[:, cols], hidden[:])
+            for b in range(2):
+                nc.tensor.matmul_mx(
+                    out=y_bank[:, b, :],
+                    lhsT=w2_codes[:, P * b : P * (b + 1)].bitcast(FP8X4),
+                    lhsT_scale=w2_scales[:, P * b : P * (b + 1)],
+                    rhs=h_codes[:].bitcast(FP8X4),
+                    rhs_scale=h_scales[:],
+                    start=True,
+                    stop=True,
+                )
+            y = small.tile([P, 2, C], F32, name="y")
+            nc.scalar.copy(out=y[:], in_=y_bank[:])
+            for b in range(2):
+                nc.vector.tensor_tensor(
+                    sums[b][:].indirect(offsets[:, 16 * e : 16 * (e + 1)]),
+                    y[:, b, :],
+                    gates[:, C * e : C * (e + 1)],
+                    MULT,
+                )
+                if e == E - 1:
+                    for q in range(2):
+                        cols = slice(640 * q, 640 * (q + 1))
+                        nc.vector.tensor_tensor(final[b][:, cols], sums[b][:, cols], residual[b][:, cols], ADD)
+                        nc.sync.dma_start(out=out[P * b : P * (b + 1), cols], in_=final[b][:, cols])

@@ -21,22 +21,29 @@ ADD = mybir.AluOpType.add
 
 P = 128
 PASSES = K // 512
-X_CHUNKS = ((0, 256), (256, 512), (768, 512))
-X_VECTOR = 1 / 8
-W1_VECTOR = 32
-W2_VECTOR = 64
-RAW_BUFS = 11
 LIST_HALF = 512
+
+X_CHUNKS = ((0, 256, 128), (256, 512, 128), (768, 512, 128))
+W1_ENGINES = (("S", "S", "S"), ("S", "V", "S"), ("S", "V", "S"), ("S", "SV", "SV"))
+W2_VECTOR = 192
+T_ORDER = (2, 3, 0, 1)
+LIVE = {"rows": 10, "w2_rows": 3}
+LAG_QUANTIZE = 1
+LAG_GELU = 2
+LAG_HIDDEN = 3
+LAG_LEAVE = 5
+LAG_SCATTER = (6, 8)
 
 
 def tile_moe_res_mlp_gelu_kernel(tc, xT, xr, w1, w2, gate, offs, out):
     nc = tc.nc
     with ExitStack() as ctx:
         keep = ctx.enter_context(tc.tile_pool(name="keep", bufs=1))
-        raw_pool = ctx.enter_context(tc.tile_pool(name="raw_pool", bufs=RAW_BUFS))
-        stage = ctx.enter_context(tc.tile_pool(name="stage", bufs=4))
+        rows_pool = ctx.enter_context(tc.tile_pool(name="rows_pool", bufs=LIVE["rows"]))
+        w2_rows_pool = ctx.enter_context(tc.tile_pool(name="w2_rows_pool", bufs=LIVE["w2_rows"]))
+        stage = ctx.enter_context(tc.tile_pool(name="stage", bufs=5))
         w_pool = ctx.enter_context(tc.tile_pool(name="w_pool", bufs=8))
-        w2_pool = ctx.enter_context(tc.tile_pool(name="w2_pool", bufs=2))
+        w2_pool = ctx.enter_context(tc.tile_pool(name="w2_pool", bufs=3))
         small = ctx.enter_context(tc.tile_pool(name="small", bufs=3))
         psum1 = ctx.enter_context(tc.psum_pool(name="psum1", bufs=4))
         psum2 = ctx.enter_context(tc.psum_pool(name="psum2", bufs=3))
@@ -64,155 +71,186 @@ def tile_moe_res_mlp_gelu_kernel(tc, xT, xr, w1, w2, gate, offs, out):
         residual = [keep.tile([P, T], F32, name=f"residual{b}") for b in range(2)]
         final = [keep.tile([P, T], F32, name=f"final{b}") for b in range(2)]
 
+        items = [("x", s, chunk) for s in range(PASSES) for chunk in range(len(X_CHUNKS))]
+        for e in range(E):
+            items += [("w1", e, s) for s in range(PASSES)] + [("w2", e, 0)]
+        waiting = list(reversed(items))
+        live = {"rows": 0, "w2_rows": 0}
         loaded = {}
 
-        def load_x(s, chunk):
-            c0, width = X_CHUNKS[chunk]
-            raw = raw_pool.tile([P, 4, width], F32, name="raw", align_bytes=64)
-            rows = xT[512 * s : 512 * (s + 1), c0 : c0 + width]
-            nc.sync.dma_start(out=raw[:], in_=rows.rearrange("(p j) w -> p j w", j=4))
-            loaded["x", s, chunk] = raw
+        def ring(kind):
+            return "w2_rows" if kind == "w2" else "rows"
 
-        def load_w1(e, s):
-            raw = raw_pool.tile([P, 4, H], F32, name="raw", align_bytes=64)
-            rows = w1[e, 512 * s : 512 * (s + 1), :]
-            nc.sync.dma_start(out=raw[:], in_=rows.rearrange("(p j) w -> p j w", j=4))
-            loaded["w1", e, s] = raw
+        def load_ahead():
+            while waiting and live[ring(waiting[-1][0])] < LIVE[ring(waiting[-1][0])]:
+                item = waiting.pop()
+                kind = item[0]
+                if kind == "x":
+                    c0, width, cut = X_CHUNKS[item[2]]
+                    rows = xT[512 * item[1] : 512 * (item[1] + 1), c0 : c0 + width]
+                elif kind == "w1":
+                    rows = w1[item[1], 512 * item[2] : 512 * (item[2] + 1), :]
+                else:
+                    rows = w2[item[1]]
+                pool = w2_rows_pool if kind == "w2" else rows_pool
+                raw = pool.tile([P, 4, rows.shape[1]], F32, name=ring(kind), align_bytes=64)
+                nc.sync.dma_start(out=raw[:], in_=rows.rearrange("(p j) w -> p j w", j=4))
+                loaded[item] = raw
+                live[ring(kind)] += 1
+                if item == ("w2", 0, 0):
+                    nc.sync.dma_start(out=gates[:], in_=gate[0:P, :])
+                if not waiting:
+                    for b in range(2):
+                        nc.sync.dma_start(out=residual[b][:], in_=xr[P * b : P * (b + 1), :])
 
-        def load_w2(e):
-            raw = w2_pool.tile([P, 4, N], F32, name="raw2", align_bytes=64)
-            nc.sync.dma_start(out=raw[:], in_=w2[e].rearrange("(p j) w -> p j w", j=4))
-            loaded["w2", e] = raw
+        grouped = {}
+        weights = {}
+        hidden = {}
+        banks = {}
+        results = {}
 
-        def load_gate():
-            nc.sync.dma_start(out=gates[:], in_=gate[0:P, :])
+        def copy(engine, dst, src):
+            if engine == "V":
+                nc.vector.tensor_copy(out=dst, in_=src)
+            else:
+                nc.scalar.activation(out=dst, in_=src, func=COPY)
 
-        def load_xr(b):
-            nc.sync.dma_start(out=residual[b][:], in_=xr[P * b : P * (b + 1), :])
+        def interleave(item):
+            kind = item[0]
+            raw = loaded.pop(item)
+            live[ring(kind)] -= 1
+            grouped[item] = []
+            if kind == "w1":
+                engines = W1_ENGINES[item[1]][item[2]]
+                ts = 4 // len(engines)
+                src = raw[:].rearrange("p j (m t) -> p m j t", t=4)
+                for i, engine in enumerate(engines):
+                    wide = stage.tile([P, 4 * P * ts], BF16, name=f"grouped{P * ts}", align_bytes=64)
+                    dst = wide[:].rearrange("p (t m j) -> p m j t", t=ts, j=4)
+                    copy(engine, dst, src[:, :, :, ts * i : ts * (i + 1)])
+                    grouped[item].append(wide)
+            else:
+                width = raw.shape[2]
+                cut = (X_CHUNKS[item[2]][2] if kind == "x" else W2_VECTOR) // 4
+                wide = stage.tile([P, 4 * width], BF16, name=f"grouped{width}", align_bytes=64)
+                dst = wide[:].rearrange("p (c i j) -> p c j i", i=4, j=4)
+                src = raw[:].rearrange("p j (c i) -> p c j i", i=4)
+                copy("S", dst[:, cut:], src[:, cut:])
+                if cut:
+                    copy("V", dst[:, :cut], src[:, :cut])
+                grouped[item].append(wide)
 
-        loads = []
-        for s in range(PASSES):
-            for chunk in range(3):
-                loads.append((load_x, s, chunk))
-        for e in range(E):
-            for s in range(PASSES):
-                loads.append((load_w1, e, s))
-            loads.append((load_w2, e))
-            if e == 0:
-                loads.append((load_gate,))
-        loads.append((load_xr, 0))
-        loads.append((load_xr, 1))
-        loads.reverse()
+        def quantize(item):
+            kind, e, s = item
+            if kind == "x":
+                c0, width, cut = X_CHUNKS[s]
+                codes, scales = x_codes[e][:, c0 : c0 + width], x_scales[4 * e : P, c0 : c0 + width]
+            elif kind == "w1":
+                w1_codes = w_pool.tile([P, H], U32, name="w1_codes", align_bytes=64)
+                w1_scales = w_pool.tile([P, H], U8, name="w1_scales", align_bytes=64)
+                weights[item] = (w1_codes, w1_scales)
+                codes, scales = w1_codes[:], w1_scales[:]
+            else:
+                w2_codes = w2_pool.tile([P, N], U32, name="w2_codes", align_bytes=64)
+                w2_scales = w2_pool.tile([P, N], U8, name="w2_scales", align_bytes=64)
+                weights[item] = (w2_codes, w2_scales)
+                codes, scales = w2_codes[:], w2_scales[:]
+            pieces = grouped.pop(item)
+            width = codes.shape[1] // len(pieces)
+            for i in reversed(range(len(pieces))):
+                cols = slice(width * i, width * (i + 1))
+                nc.vector.quantize_mx(out=codes[:, cols].bitcast(FP8X4), scales=scales[:, cols], in_=pieces[i][:])
 
-        def issue(count):
-            for i in range(min(count, len(loads))):
-                call = loads.pop()
-                call[0](*call[1:])
+        def gather(target, window, f):
+            nc.vector.tensor_copy(target[f][:], window[:].indirect(offsets[:, 32 * f : 32 * (f + 1)]))
 
-        def split_copy(dst, src, cut):
-            if cut > 0:
-                nc.vector.tensor_copy(out=dst[:, :cut], in_=src[:, :cut])
-            nc.scalar.activation(out=dst[:, cut:], in_=src[:, cut:], func=COPY)
-
-        def quantize(codes, scales, grouped):
-            nc.vector.quantize_mx(out=codes.bitcast(FP8X4), scales=scales, in_=grouped)
-
-        issue(RAW_BUFS - 1)
-        for s in range(PASSES):
-            for chunk in range(3):
-                c0, width = X_CHUNKS[chunk]
-                raw = loaded.pop(("x", s, chunk))
-                grouped = stage.tile([P, 4 * width], BF16, name="grouped", align_bytes=64)
-                split_copy(
-                    grouped[:].rearrange("p (c i t) -> p c t i", i=4, t=4),
-                    raw[:].rearrange("p t (c i) -> p c t i", i=4),
-                    int(width // 4 * X_VECTOR),
-                )
-                quantize(x_codes[s][:, c0 : c0 + width], x_scales[4 * s : P, c0 : c0 + width], grouped[:])
-                issue(1)
-            for f in range(2):
-                picked = offsets[:, 32 * f : 32 * (f + 1)]
-                nc.vector.tensor_copy(g_codes[s][f][:], x_codes[s][:].indirect(picked))
-        for f in range(2):
-            picked = offsets[:, 32 * f : 32 * (f + 1)]
-            nc.vector.tensor_copy(g_scales[f][:], x_scales[:].indirect(picked))
-
-        for e in range(E):
-            w1_codes = []
-            w1_scales = []
-            for s in range(PASSES):
-                raw = loaded.pop(("w1", e, s))
-                grouped = stage.tile([P, 4 * H], BF16, name="grouped", align_bytes=64)
-                split_copy(
-                    grouped[:].rearrange("p (t m j) -> p m j t", t=4, j=4),
-                    raw[:].rearrange("p j (m t) -> p m j t", t=4),
-                    W1_VECTOR,
-                )
-                codes = w_pool.tile([P, H], U32, name="w1_codes", align_bytes=64)
-                scales = w_pool.tile([P, H], U8, name="w1_scales", align_bytes=64)
-                quantize(codes[:], scales[:], grouped[:])
-                w1_codes.append(codes)
-                w1_scales.append(scales)
-                issue(1)
-            raw = loaded.pop(("w2", e))
-            grouped2 = stage.tile([P, 4 * N], BF16, name="grouped2", align_bytes=64)
-            split_copy(
-                grouped2[:].rearrange("p (c i j) -> p c j i", i=4, j=4),
-                raw[:].rearrange("p j (c i) -> p c j i", i=4),
-                W2_VECTOR // 4,
+        def first_layer(e, part):
+            f, at = divmod(C * e + P * part, LIST_HALF)
+            a_bank = psum1.tile([P, 4, P], F32, name="a_bank")
+            for t in T_ORDER:
+                rows = slice(P * t, P * (t + 1))
+                for s in range(PASSES):
+                    codes, scales = weights["w1", e, s]
+                    nc.tensor.matmul_mx(
+                        out=a_bank[:, t, :],
+                        lhsT=codes[:, rows].bitcast(FP8X4),
+                        lhsT_scale=scales[:, rows],
+                        rhs=g_codes[s][f][:, at : at + P].bitcast(FP8X4),
+                        rhs_scale=g_scales[f][4 * s : P, at : at + P],
+                        start=(s == 0),
+                        stop=(s == PASSES - 1),
+                    )
+            h = small.tile([P, 4 * P], BF16, name="h", align_bytes=64)
+            nc.scalar.activation(
+                out=h[:].rearrange("p (n t) -> p n t", t=4), in_=a_bank[:].rearrange("p t n -> p n t"), func=GELU
             )
-            w2_codes = w2_pool.tile([P, N], U32, name="w2_codes", align_bytes=64)
-            w2_scales = w2_pool.tile([P, N], U8, name="w2_scales", align_bytes=64)
-            quantize(w2_codes[:], w2_scales[:], grouped2[:])
-            issue(2)
+            hidden[e, part] = h
 
-            y_bank = psum2.tile([P, 2, C], F32, name="y_bank")
+        def second_layer(e):
             h_codes = small.tile([P, C], U32, name="h_codes", align_bytes=64)
             h_scales = small.tile([P, C], U8, name="h_scales", align_bytes=64)
             for part in range(2):
-                slot = C * e + 128 * part
-                f, at = divmod(slot, LIST_HALF)
-                a_bank = psum1.tile([P, 4, 128], F32, name="a_bank")
-                for t in range(4):
-                    for s in range(PASSES):
-                        nc.tensor.matmul_mx(
-                            out=a_bank[:, t, :],
-                            lhsT=w1_codes[s][:, 128 * t : 128 * (t + 1)].bitcast(FP8X4),
-                            lhsT_scale=w1_scales[s][:, 128 * t : 128 * (t + 1)],
-                            rhs=g_codes[s][f][:, at : at + 128].bitcast(FP8X4),
-                            rhs_scale=g_scales[f][4 * s : P, at : at + 128],
-                            start=(s == 0),
-                            stop=(s == PASSES - 1),
-                        )
-                hidden = small.tile([P, 512], BF16, name="hidden", align_bytes=64)
-                nc.scalar.activation(
-                    out=hidden[:].rearrange("p (n t) -> p n t", t=4),
-                    in_=a_bank[:].rearrange("p t n -> p n t"),
-                    func=GELU,
+                cols = slice(P * part, P * (part + 1))
+                nc.vector.quantize_mx(
+                    out=h_codes[:, cols].bitcast(FP8X4), scales=h_scales[:, cols], in_=hidden[e, part][:]
                 )
-                cols = slice(128 * part, 128 * (part + 1))
-                quantize(h_codes[:, cols], h_scales[:, cols], hidden[:])
+            codes, scales = weights["w2", e, 0]
+            y_bank = psum2.tile([P, 2, C], F32, name="y_bank")
             for b in range(2):
+                rows = slice(P * b, P * (b + 1))
                 nc.tensor.matmul_mx(
                     out=y_bank[:, b, :],
-                    lhsT=w2_codes[:, P * b : P * (b + 1)].bitcast(FP8X4),
-                    lhsT_scale=w2_scales[:, P * b : P * (b + 1)],
+                    lhsT=codes[:, rows].bitcast(FP8X4),
+                    lhsT_scale=scales[:, rows],
                     rhs=h_codes[:].bitcast(FP8X4),
                     rhs_scale=h_scales[:],
                     start=True,
                     stop=True,
                 )
+            banks[e] = y_bank
+
+        def leave_bank(e):
             y = small.tile([P, 2, C], F32, name="y")
-            nc.scalar.copy(out=y[:], in_=y_bank[:])
             for b in range(2):
-                nc.vector.tensor_tensor(
-                    sums[b][:].indirect(offsets[:, 16 * e : 16 * (e + 1)]),
-                    y[:, b, :],
-                    gates[:, C * e : C * (e + 1)],
-                    MULT,
-                )
-                if e == E - 1:
-                    for q in range(2):
-                        cols = slice(640 * q, 640 * (q + 1))
-                        nc.vector.tensor_tensor(final[b][:, cols], sums[b][:, cols], residual[b][:, cols], ADD)
-                        nc.sync.dma_start(out=out[P * b : P * (b + 1), cols], in_=final[b][:, cols])
+                nc.scalar.copy(out=y[:, b, :], in_=banks[e][:, b, :])
+            results[e] = y
+
+        def put_back(e, b):
+            nc.vector.tensor_tensor(
+                sums[b][:].indirect(offsets[:, 16 * e : 16 * (e + 1)]),
+                results[e][:, b, :],
+                gates[:, C * e : C * (e + 1)],
+                MULT,
+            )
+
+        load_ahead()
+        for step in range(len(items) + LAG_SCATTER[1]):
+            if step < len(items):
+                interleave(items[step])
+                load_ahead()
+            if LAG_QUANTIZE <= step < len(items) + LAG_QUANTIZE:
+                item = items[step - LAG_QUANTIZE]
+                quantize(item)
+                if item[0] == "x" and item[2] == len(X_CHUNKS) - 1:
+                    for f in range(2):
+                        gather(g_codes[item[1]], x_codes[item[1]], f)
+                        if item[1] == PASSES - 1:
+                            gather(g_scales, x_scales, f)
+            for e in range(E):
+                if step - items.index(("w2", e, 0)) == LAG_GELU:
+                    first_layer(e, 0)
+                    first_layer(e, 1)
+            for e in range(E):
+                lag = step - items.index(("w2", e, 0))
+                if lag == LAG_HIDDEN:
+                    second_layer(e)
+                if lag == LAG_LEAVE:
+                    leave_bank(e)
+                for b in range(2):
+                    if lag == LAG_SCATTER[b]:
+                        put_back(e, b)
+        for b in range(2):
+            for q in range(2):
+                cols = slice(640 * q, 640 * (q + 1))
+                nc.vector.tensor_tensor(final[b][:, cols], sums[b][:, cols], residual[b][:, cols], ADD)
+                nc.sync.dma_start(out=out[P * b : P * (b + 1), cols], in_=final[b][:, cols])

@@ -23,9 +23,8 @@ P = 128
 PASSES = K // 512
 LIST_HALF = 512
 
-X_CHUNKS = ((0, 256, 128), (256, 512, 128), (768, 512, 128))
-W1_ENGINES = (("S", "S", "S"), ("S", "V", "S"), ("S", "V", "S"), ("S", "SV", "SV"))
-W2_VECTOR = 192
+X_CHUNKS = ((0, 256, "V"), (256, 512, "S"), (768, 512, "S"))
+W1_ENGINES = (("S", "S", "SV"), ("S", "SV", "S"), ("S", "SV", "S"), ("S", "SV", "SV"))
 T_ORDER = (2, 3, 0, 1)
 LIVE = {"rows": 10, "w2_rows": 3}
 LAG_QUANTIZE = 1
@@ -41,7 +40,7 @@ def tile_moe_res_mlp_gelu_kernel(tc, xT, xr, w1, w2, gate, offs, out):
         keep = ctx.enter_context(tc.tile_pool(name="keep", bufs=1))
         rows_pool = ctx.enter_context(tc.tile_pool(name="rows_pool", bufs=LIVE["rows"]))
         w2_rows_pool = ctx.enter_context(tc.tile_pool(name="w2_rows_pool", bufs=LIVE["w2_rows"]))
-        stage = ctx.enter_context(tc.tile_pool(name="stage", bufs=5))
+        stage = ctx.enter_context(tc.tile_pool(name="stage", bufs=4))
         w_pool = ctx.enter_context(tc.tile_pool(name="w_pool", bufs=8))
         w2_pool = ctx.enter_context(tc.tile_pool(name="w2_pool", bufs=3))
         small = ctx.enter_context(tc.tile_pool(name="small", bufs=3))
@@ -73,7 +72,10 @@ def tile_moe_res_mlp_gelu_kernel(tc, xT, xr, w1, w2, gate, offs, out):
 
         items = [("x", s, chunk) for s in range(PASSES) for chunk in range(len(X_CHUNKS))]
         for e in range(E):
-            items += [("w1", e, s) for s in range(PASSES)] + [("w2", e, 0)]
+            first = [("w1", e, s) for s in range(PASSES)]
+            second = [("w2", e, 0)]
+            items += second + first if e == 0 else first + second
+        last_item = [len(items) - (PASSES + 1) * (E - 1 - e) - 1 for e in range(E)]
         waiting = list(reversed(items))
         live = {"rows": 0, "w2_rows": 0}
         loaded = {}
@@ -86,7 +88,7 @@ def tile_moe_res_mlp_gelu_kernel(tc, xT, xr, w1, w2, gate, offs, out):
                 item = waiting.pop()
                 kind = item[0]
                 if kind == "x":
-                    c0, width, cut = X_CHUNKS[item[2]]
+                    c0, width, engine = X_CHUNKS[item[2]]
                     rows = xT[512 * item[1] : 512 * (item[1] + 1), c0 : c0 + width]
                 elif kind == "w1":
                     rows = w1[item[1], 512 * item[2] : 512 * (item[2] + 1), :]
@@ -131,19 +133,16 @@ def tile_moe_res_mlp_gelu_kernel(tc, xT, xr, w1, w2, gate, offs, out):
                     grouped[item].append(wide)
             else:
                 width = raw.shape[2]
-                cut = (X_CHUNKS[item[2]][2] if kind == "x" else W2_VECTOR) // 4
                 wide = stage.tile([P, 4 * width], BF16, name=f"grouped{width}", align_bytes=64)
                 dst = wide[:].rearrange("p (c i j) -> p c j i", i=4, j=4)
                 src = raw[:].rearrange("p j (c i) -> p c j i", i=4)
-                copy("S", dst[:, cut:], src[:, cut:])
-                if cut:
-                    copy("V", dst[:, :cut], src[:, :cut])
+                copy(X_CHUNKS[item[2]][2] if kind == "x" else "V", dst, src)
                 grouped[item].append(wide)
 
         def quantize(item):
             kind, e, s = item
             if kind == "x":
-                c0, width, cut = X_CHUNKS[s]
+                c0, width, engine = X_CHUNKS[s]
                 codes, scales = x_codes[e][:, c0 : c0 + width], x_scales[4 * e : P, c0 : c0 + width]
             elif kind == "w1":
                 w1_codes = w_pool.tile([P, H], U32, name="w1_codes", align_bytes=64)
@@ -237,11 +236,11 @@ def tile_moe_res_mlp_gelu_kernel(tc, xT, xr, w1, w2, gate, offs, out):
                         if item[1] == PASSES - 1:
                             gather(g_scales, x_scales, f)
             for e in range(E):
-                if step - items.index(("w2", e, 0)) == LAG_GELU:
+                if step - last_item[e] == LAG_GELU:
                     first_layer(e, 0)
                     first_layer(e, 1)
             for e in range(E):
-                lag = step - items.index(("w2", e, 0))
+                lag = step - last_item[e]
                 if lag == LAG_HIDDEN:
                     second_layer(e)
                 if lag == LAG_LEAVE:

from contextlib import ExitStack

import concourse.mybir as mybir

K, T, E, C, H, N = 1536, 1280, 4, 256, 512, 256
S = E * C

FLOPS = 2 * S * K * H + 2 * S * H * N
BYTES = 4 * (K * T + 2 * N * T + E * K * H + E * H * N + 128 * S) + 2 * 128 * (S // 16)

F32 = mybir.dt.float32
BF16 = mybir.dt.bfloat16
U32 = mybir.dt.uint32
U16 = mybir.dt.uint16
U8 = mybir.dt.uint8
FP8X4 = mybir.dt.float8_e4m3fn_x4
COPY = mybir.ActivationFunctionType.Copy
GELU = mybir.ActivationFunctionType.Gelu_apprx_tanh
MULT = mybir.AluOpType.mult
ADD = mybir.AluOpType.add

P = 128
PASSES = K // 512
LIST_HALF = 512

X_CHUNKS = ((0, 256, "V"), (256, 512, "S"), (768, 512, "S"))
W1_ENGINES = (("S", "S", "SV"), ("S", "SV", "S"), ("S", "SV", "S"), ("S", "SV", "SV"))
T_ORDER = (2, 3, 0, 1)
LIVE = {"rows": 10, "w2_rows": 3}
LAG_QUANTIZE = 1
LAG_GELU = 2
LAG_HIDDEN = 3
LAG_LEAVE = 5
LAG_SCATTER = (6, 8)


def tile_moe_res_mlp_gelu_kernel(tc, xT, xr, w1, w2, gate, offs, out):
    nc = tc.nc
    with ExitStack() as ctx:
        keep = ctx.enter_context(tc.tile_pool(name="keep", bufs=1))
        rows_pool = ctx.enter_context(tc.tile_pool(name="rows_pool", bufs=LIVE["rows"]))
        w2_rows_pool = ctx.enter_context(tc.tile_pool(name="w2_rows_pool", bufs=LIVE["w2_rows"]))
        stage = ctx.enter_context(tc.tile_pool(name="stage", bufs=4))
        w_pool = ctx.enter_context(tc.tile_pool(name="w_pool", bufs=8))
        w2_pool = ctx.enter_context(tc.tile_pool(name="w2_pool", bufs=3))
        small = ctx.enter_context(tc.tile_pool(name="small", bufs=3))
        psum1 = ctx.enter_context(tc.psum_pool(name="psum1", bufs=4))
        psum2 = ctx.enter_context(tc.psum_pool(name="psum2", bufs=3))

        offsets = keep.tile([P, S // 16], U16, name="offsets")
        nc.sync.dma_start(offsets[:], offs)

        warm = keep.tile([P, 2], F32, name="warm")
        nc.vector.memset(warm[:], 0.0)
        nc.scalar.activation(out=warm[:, 1:2], in_=warm[:, 0:1], func=GELU)

        x_scales = keep.tile([P, T], U8, name="x_scales", align_bytes=64)
        nc.gpsimd.memset(x_scales[:], 0)
        sums = [keep.tile([P, T], F32, name=f"sums{b}") for b in range(2)]
        for b in range(2):
            nc.vector.memset(sums[b][:], 0.0)

        x_codes = [keep.tile([P, T], U32, name=f"x_codes{s}", align_bytes=64) for s in range(PASSES)]
        g_codes = [
            [keep.tile([P, LIST_HALF], U32, name=f"g_codes{s}_{f}", align_bytes=64) for f in range(2)]
            for s in range(PASSES)
        ]
        g_scales = [keep.tile([P, LIST_HALF], U8, name=f"g_scales{f}", align_bytes=64) for f in range(2)]
        gates = keep.tile([P, S], F32, name="gates")
        residual = [keep.tile([P, T], F32, name=f"residual{b}") for b in range(2)]
        final = [keep.tile([P, T], F32, name=f"final{b}") for b in range(2)]

        items = [("x", s, chunk) for s in range(PASSES) for chunk in range(len(X_CHUNKS))]
        for e in range(E):
            first = [("w1", e, s) for s in range(PASSES)]
            second = [("w2", e, 0)]
            items += second + first if e == 0 else first + second
        last_item = [len(items) - (PASSES + 1) * (E - 1 - e) - 1 for e in range(E)]
        waiting = list(reversed(items))
        live = {"rows": 0, "w2_rows": 0}
        loaded = {}

        def ring(kind):
            return "w2_rows" if kind == "w2" else "rows"

        def load_ahead():
            while waiting and live[ring(waiting[-1][0])] < LIVE[ring(waiting[-1][0])]:
                item = waiting.pop()
                kind = item[0]
                if kind == "x":
                    c0, width, engine = X_CHUNKS[item[2]]
                    rows = xT[512 * item[1] : 512 * (item[1] + 1), c0 : c0 + width]
                elif kind == "w1":
                    rows = w1[item[1], 512 * item[2] : 512 * (item[2] + 1), :]
                else:
                    rows = w2[item[1]]
                pool = w2_rows_pool if kind == "w2" else rows_pool
                raw = pool.tile([P, 4, rows.shape[1]], F32, name=ring(kind), align_bytes=64)
                nc.sync.dma_start(out=raw[:], in_=rows.rearrange("(p j) w -> p j w", j=4))
                loaded[item] = raw
                live[ring(kind)] += 1
                if item == ("w2", 0, 0):
                    nc.sync.dma_start(out=gates[:], in_=gate[0:P, :])
                if not waiting:
                    for b in range(2):
                        nc.sync.dma_start(out=residual[b][:], in_=xr[P * b : P * (b + 1), :])

        grouped = {}
        weights = {}
        hidden = {}
        banks = {}
        results = {}

        def copy(engine, dst, src):
            if engine == "V":
                nc.vector.tensor_copy(out=dst, in_=src)
            else:
                nc.scalar.activation(out=dst, in_=src, func=COPY)

        def interleave(item):
            kind = item[0]
            raw = loaded.pop(item)
            live[ring(kind)] -= 1
            grouped[item] = []
            if kind == "w1":
                engines = W1_ENGINES[item[1]][item[2]]
                ts = 4 // len(engines)
                src = raw[:].rearrange("p j (m t) -> p m j t", t=4)
                for i, engine in enumerate(engines):
                    wide = stage.tile([P, 4 * P * ts], BF16, name=f"grouped{P * ts}", align_bytes=64)
                    dst = wide[:].rearrange("p (t m j) -> p m j t", t=ts, j=4)
                    copy(engine, dst, src[:, :, :, ts * i : ts * (i + 1)])
                    grouped[item].append(wide)
            else:
                width = raw.shape[2]
                wide = stage.tile([P, 4 * width], BF16, name=f"grouped{width}", align_bytes=64)
                dst = wide[:].rearrange("p (c i j) -> p c j i", i=4, j=4)
                src = raw[:].rearrange("p j (c i) -> p c j i", i=4)
                copy(X_CHUNKS[item[2]][2] if kind == "x" else "V", dst, src)
                grouped[item].append(wide)

        def quantize(item):
            kind, e, s = item
            if kind == "x":
                c0, width, engine = X_CHUNKS[s]
                codes, scales = x_codes[e][:, c0 : c0 + width], x_scales[4 * e : P, c0 : c0 + width]
            elif kind == "w1":
                w1_codes = w_pool.tile([P, H], U32, name="w1_codes", align_bytes=64)
                w1_scales = w_pool.tile([P, H], U8, name="w1_scales", align_bytes=64)
                weights[item] = (w1_codes, w1_scales)
                codes, scales = w1_codes[:], w1_scales[:]
            else:
                w2_codes = w2_pool.tile([P, N], U32, name="w2_codes", align_bytes=64)
                w2_scales = w2_pool.tile([P, N], U8, name="w2_scales", align_bytes=64)
                weights[item] = (w2_codes, w2_scales)
                codes, scales = w2_codes[:], w2_scales[:]
            pieces = grouped.pop(item)
            width = codes.shape[1] // len(pieces)
            for i in reversed(range(len(pieces))):
                cols = slice(width * i, width * (i + 1))
                nc.vector.quantize_mx(out=codes[:, cols].bitcast(FP8X4), scales=scales[:, cols], in_=pieces[i][:])

        def gather(target, window, f):
            nc.vector.tensor_copy(target[f][:], window[:].indirect(offsets[:, 32 * f : 32 * (f + 1)]))

        def first_layer(e, part):
            f, at = divmod(C * e + P * part, LIST_HALF)
            a_bank = psum1.tile([P, 4, P], F32, name="a_bank")
            for t in T_ORDER:
                rows = slice(P * t, P * (t + 1))
                for s in range(PASSES):
                    codes, scales = weights["w1", e, s]
                    nc.tensor.matmul_mx(
                        out=a_bank[:, t, :],
                        lhsT=codes[:, rows].bitcast(FP8X4),
                        lhsT_scale=scales[:, rows],
                        rhs=g_codes[s][f][:, at : at + P].bitcast(FP8X4),
                        rhs_scale=g_scales[f][4 * s : P, at : at + P],
                        start=(s == 0),
                        stop=(s == PASSES - 1),
                    )
            h = small.tile([P, 4 * P], BF16, name="h", align_bytes=64)
            nc.scalar.activation(
                out=h[:].rearrange("p (n t) -> p n t", t=4), in_=a_bank[:].rearrange("p t n -> p n t"), func=GELU
            )
            hidden[e, part] = h

        def second_layer(e):
            h_codes = small.tile([P, C], U32, name="h_codes", align_bytes=64)
            h_scales = small.tile([P, C], U8, name="h_scales", align_bytes=64)
            for part in range(2):
                cols = slice(P * part, P * (part + 1))
                nc.vector.quantize_mx(
                    out=h_codes[:, cols].bitcast(FP8X4), scales=h_scales[:, cols], in_=hidden[e, part][:]
                )
            codes, scales = weights["w2", e, 0]
            y_bank = psum2.tile([P, 2, C], F32, name="y_bank")
            for b in range(2):
                rows = slice(P * b, P * (b + 1))
                nc.tensor.matmul_mx(
                    out=y_bank[:, b, :],
                    lhsT=codes[:, rows].bitcast(FP8X4),
                    lhsT_scale=scales[:, rows],
                    rhs=h_codes[:].bitcast(FP8X4),
                    rhs_scale=h_scales[:],
                    start=True,
                    stop=True,
                )
            banks[e] = y_bank

        def leave_bank(e):
            y = small.tile([P, 2, C], F32, name="y")
            for b in range(2):
                nc.scalar.copy(out=y[:, b, :], in_=banks[e][:, b, :])
            results[e] = y

        def put_back(e, b):
            nc.vector.tensor_tensor(
                sums[b][:].indirect(offsets[:, 16 * e : 16 * (e + 1)]),
                results[e][:, b, :],
                gates[:, C * e : C * (e + 1)],
                MULT,
            )

        load_ahead()
        for step in range(len(items) + LAG_SCATTER[1]):
            if step < len(items):
                interleave(items[step])
                load_ahead()
            if LAG_QUANTIZE <= step < len(items) + LAG_QUANTIZE:
                item = items[step - LAG_QUANTIZE]
                quantize(item)
                if item[0] == "x" and item[2] == len(X_CHUNKS) - 1:
                    for f in range(2):
                        gather(g_codes[item[1]], x_codes[item[1]], f)
                        if item[1] == PASSES - 1:
                            gather(g_scales, x_scales, f)
            for e in range(E):
                if step - last_item[e] == LAG_GELU:
                    first_layer(e, 0)
                    first_layer(e, 1)
            for e in range(E):
                lag = step - last_item[e]
                if lag == LAG_HIDDEN:
                    second_layer(e)
                if lag == LAG_LEAVE:
                    leave_bank(e)
                for b in range(2):
                    if lag == LAG_SCATTER[b]:
                        put_back(e, b)
        for b in range(2):
            for q in range(2):
                cols = slice(640 * q, 640 * (q + 1))
                nc.vector.tensor_tensor(final[b][:, cols], sums[b][:, cols], residual[b][:, cols], ADD)
                nc.sync.dma_start(out=out[P * b : P * (b + 1), cols], in_=final[b][:, cols])
